import numpy as np
import ml_dtypes


def mxq(x, axis, fmt="e4m3"):
    dtype, down = {"e4m3": (ml_dtypes.float8_e4m3fn, 7), "e5m2": (ml_dtypes.float8_e5m2, 14)}[fmt]
    v = np.moveaxis(np.asarray(x, np.float32).astype(ml_dtypes.bfloat16).astype(np.float64), axis, -1)
    blocks = v.reshape(v.shape[:-1] + (-1, 32))
    amax = np.abs(blocks).max(-1, keepdims=True)
    byte = np.maximum(np.where(amax > 0, np.frexp(amax)[1] - 1 + 127, 0) - down, 1)
    scale = np.exp2(byte - 127.0)
    codes = (blocks / scale).astype(np.float32).astype(dtype).astype(np.float64)
    return np.moveaxis((codes * scale).reshape(v.shape), -1, axis)


WIDE = False


def mx_kscale(k):
    if not WIDE:
        return np.ones(k)
    levels = np.array([10, -10, 5, -5, 0])
    if k % 512:
        return np.exp2(np.random.permutation(np.resize(levels, k // 32))).repeat(32)
    a = np.empty((k // 512, 16))
    for p in range(k // 512):
        a[p, :8] = np.random.permutation(np.resize(levels, 8))
        for g in range(8):
            far = levels[np.abs(levels - a[p, g]) >= 10]
            a[p, g + 8] = far[np.random.randint(len(far))]
    return np.exp2(a.ravel()).repeat(32)


def f64(x):
    return np.asarray(x).astype(np.float64)


def striped(idx):
    return np.tile(idx.reshape(-1, 16).T, (8, 1)).astype(np.uint16)


def unstriped(offs):
    return offs[:16].T.reshape(-1).astype(np.int64)


def striped8(idx):
    return np.concatenate([x.reshape(-1, 16).T for x in idx]).astype(np.uint16)


def runs(offs, k):
    lists = np.stack([offs[16 * r : 16 * r + 16].T.reshape(-1) for r in range(8)]).astype(np.int64)
    return lists[np.arange(k) % 512 // 64]


def pack_weight(w):
    k, n = w.shape
    w = f64(np.asarray(w, np.float32).astype(ml_dtypes.bfloat16)).reshape(k // 32, 32, n)
    amax = np.abs(w).max(1)
    byte = np.clip(np.where(amax > 0, np.frexp(amax)[1] - 1 + 127 - 7, 1), 1, 254)
    scaled = (w * np.exp2(127.0 - byte)[:, None, :]).reshape(k, n).astype(np.float32)
    words = np.ascontiguousarray(scaled.reshape(k // 512, 128, 4, n).transpose(0, 1, 3, 2)).astype(ml_dtypes.float8_e4m3fn).view(np.uint8)
    return words, np.ascontiguousarray(byte.astype(np.uint8).reshape(k // 512, 16, n))


def unpack_weight(words, scales):
    g, p, n, _ = words.shape
    vals = np.ascontiguousarray(words).view(ml_dtypes.float8_e4m3fn).astype(np.float64) * np.repeat(np.exp2(scales.astype(np.float64) - 127.0), 8, axis=1)[..., None]
    return vals.transpose(0, 1, 3, 2).reshape(g * 512, n)

def planes(y):
    n, m = y.shape
    v = y.astype(np.float32).astype(ml_dtypes.bfloat16).astype(np.float64).reshape(n // 32, 32, m)
    top = np.abs(v).max(1)
    byte = np.clip(np.where(top > 0, np.frexp(top)[1] - 1 + 127 - 7, 1), 1, 254)
    codes = (v * np.exp2(127.0 - byte)[:, None, :]).reshape(n, m).astype(np.float32).astype(ml_dtypes.float8_e4m3fn).view(np.uint8)
    words = codes.reshape(n // 512, 128, 4, m).transpose(0, 1, 3, 2)
    return np.ascontiguousarray(words), np.ascontiguousarray(byte.astype(np.uint8).reshape(n // 512, 16, m))


K, T, S, G, H, W, C = 512, 1024, 512, 2048, 512, 256, 512


def setup_inputs():
    n = np.random.standard_normal
    s = mx_kscale(K)[:, None]
    packed_xT = pack_weight(n((K, T)) * s)
    packed_dT = pack_weight(n((K, G)) / s)
    perm = np.random.permutation(S)
    return {
        "x_words": packed_xT[0],
        "x_scales": packed_xT[1],
        "d_words": packed_dT[0],
        "d_scales": packed_dT[1],
        "gs": (np.random.uniform(0.5, 1.5, (K, 1)) / s).astype(np.float32),
        "offs": striped(np.random.permutation(T)[:S]),
        "k1": striped8(np.random.randint(0, G, (8, H))),
        "n1": striped(perm[:W]),
        "n2": striped(perm[W:]),
        "cand": striped(np.random.permutation(T)[:C]),
        "two": striped(np.random.permutation(T)[:S]),
        "k2": striped8(np.random.randint(0, G, (8, H))),
        "n3": striped8(np.stack([np.random.permutation(S) for _ in range(8)])),
        "n4": striped8(np.stack([np.random.permutation(S) for _ in range(8)])),
        "n5": striped8(np.stack([np.random.permutation(S) for _ in range(8)])),
    }


def reference(x_words, x_scales, d_words, d_scales, gs, offs, k1, n1, n2, cand, two, k2, n3, n4, n5):
    d_k2 = unpack_weight(d_words, d_scales)[np.arange(K)[:, None], runs(k2, K)]
    x_two = unpack_weight(x_words, x_scales)[:, unstriped(two)]
    b = 0.0625 * (d_k2.T @ x_two)
    x_cand = unpack_weight(x_words, x_scales)[:, unstriped(cand)]
    d_k1 = unpack_weight(d_words, d_scales)[np.arange(K)[:, None], runs(k1, K)]
    xq = unpack_weight(x_words, x_scales)[:, unstriped(offs)]
    h = 0.0625 * (d_k1.T @ xq)
    pa = h[:, unstriped(n1)]
    pb = h[:, unstriped(n2)]
    ra = np.maximum(pa, pb)
    ds = h.copy()
    ds[:, unstriped(n1)] = ra
    z = f64(gs) * ds
    a = 0.0625 * ((x_cand.T @ mxq(z, 0, "e4m3")))
    out_0 = b * (a[np.arange(C)[:, None], runs(n3, C)] - a) + 0.5 * ((b[np.arange(H)[:, None], runs(n5, H)]) * (a[np.arange(C)[:, None], runs(n4, C)] - a))
    return (out_0,) + planes(out_0)

from contextlib import ExitStack

import concourse.mybir as mybir

F32 = mybir.dt.float32
BF16 = mybir.dt.bfloat16
I32 = mybir.dt.int32
U32 = mybir.dt.uint32
U16 = mybir.dt.uint16
U8 = mybir.dt.uint8
FP8X4 = mybir.dt.float8_e4m3fn_x4
COPY = mybir.ActivationFunctionType.Copy
MULT = mybir.AluOpType.mult
ADD = mybir.AluOpType.add
MAX = mybir.AluOpType.max

P = 128
PACK = 4
S = 512
T = 1024
G = 2048
W = 256
FLOPS = 3 * 2 * 512 * 512 * 512


def tile_picked_pqcjflowbfill_none_po_kernel(
    tc, x_words, x_scales, d_words, d_scales, gs, offs, k1, n1, n2, cand, two, k2, n3, n4, n5, out_0, out_1, out_2
):
    nc = tc.nc
    with ExitStack() as ctx:
        lists = ctx.enter_context(tc.tile_pool(name="lists", bufs=1))
        keep = ctx.enter_context(tc.tile_pool(name="keep", bufs=1))
        psum = ctx.enter_context(tc.psum_pool(name="psum", bufs=1))

        def load_list(ap, name):
            tile = lists.tile(list(ap.shape), U16, name=name)
            nc.sync.dma_start(tile[:], ap)
            return tile

        def new(shape, dtype, name, tag=None):
            return keep.tile(shape, dtype, name=name, tag=tag or name, align_bytes=64)

        dsc = new([P, G], U8, "dsc")
        xsc = new([P, T], U8, "xsc")
        dwd = new([P, G], U32, "dwd")
        xwd = new([P, T], U32, "xwd")
        nc.vector.memset(dsc[:].bitcast(I32), 0)
        nc.vector.memset(xsc[:].bitcast(I32), 0)

        offs_t = load_list(offs, "offs_t")
        k1_t = load_list(k1, "k1_t")
        nc.sync.dma_start(xwd[:].bitcast(I32), x_words[0].rearrange("p n t -> p (n t)").bitcast(I32))
        for e in range(2):
            nc.sync.dma_start(dsc[e:P:16, :].bitcast(I32), d_scales[0, e:16:2, :].bitcast(I32))
        nc.sync.dma_start(dwd[:].bitcast(I32), d_words[0].rearrange("p n t -> p (n t)").bitcast(I32))
        for j in range(4):
            nc.sync.dma_start(xsc[j:P:32, :].bitcast(I32), x_scales[0, j:16:4, :].bitcast(I32))
        gs_t = new([P, PACK], F32, "gs_t")
        nc.sync.dma_start(gs_t[:], gs.rearrange("(p t) o -> p (t o)", t=PACK))
        n1_t = load_list(n1, "n1_t")
        n2_t = load_list(n2, "n2_t")
        k2_t = load_list(k2, "k2_t")
        two_t = load_list(two, "two_t")
        cand_t = load_list(cand, "cand_t")
        n5_t = load_list(n5, "n5_t")
        n3_t = load_list(n3, "n3_t")
        n4_t = load_list(n4, "n4_t")

        gs16 = new([P, PACK], F32, "gs16")
        nc.scalar.activation(gs16[:], gs_t[:], COPY, scale=0.0625)

        def gather(table, offsets, dtype, name):
            picked = new([P, S], dtype, name)
            nc.vector.tensor_copy(picked[:], table[:].indirect(offsets[:]))
            return picked

        def deal(picked, dtype, name):
            dealt = new([P, S], dtype, name)
            nc.vector.tensor_copy(
                dealt[:].rearrange("p (t m) -> p m t", t=PACK), picked[:].rearrange("p (m t) -> p m t", t=PACK)
            )
            return dealt

        def place_odd_rows(plane, queue):
            for e in range(2):
                queue.dma_start(plane[2 + e : P : 32, :].bitcast(I32), plane[16 + e : P : 32, :].bitcast(I32))

        def product(bank, lw, ls, t, rw, rs):
            cols = slice(t * P, (t + 1) * P)
            nc.tensor.matmul_mx(
                out=bank[:], lhsT=lw[:, cols].bitcast(FP8X4), lhsT_scale=ls[:, cols],
                rhs=rw[:].bitcast(FP8X4), rhs_scale=rs[:], start=True, stop=True,
            )

        def vgather(out, window, offsets):
            nc.vector.tensor_copy(out, window[:].indirect(offsets[:]))

        def sgather(out, window, offsets):
            nc.scalar.activation(out, window[:].indirect(offsets[:]), COPY)

        q_w = gather(xwd, offs_t, U32, "q_w")
        k1_s = deal(gather(dsc, k1_t, U8, "k1_sg"), U8, "k1_s")
        place_odd_rows(k1_s, nc.scalar)
        k1_w = deal(gather(dwd, k1_t, U32, "k1_wg"), U32, "k1_w")
        q_s = gather(xsc, offs_t, U8, "q_s")
        h_ps = [psum.tile([P, S], F32, name=f"ha{t}", tag=f"ha{t}") for t in range(PACK)]
        for t in range(PACK):
            product(h_ps[t], k1_w, k1_s, t, q_w, q_s)

        h_sb = [new([P, S], F32, f"h{t}") for t in range(PACK)]
        b_win = [new([P, 2 * S], F32, f"bwin{t}") for t in range(PACK)]
        ra = [new([P, W], F32, f"ra{t}") for t in range(PACK)]
        z16 = new([P, PACK, S], BF16, "z16")

        for t in range(PACK):
            nc.scalar.activation(h_sb[t][:], h_ps[t][:], COPY)
            sgather(b_win[t][:, S : S + W], h_sb[t], n1_t)
            sgather(b_win[t][:, S + W :], h_sb[t], n2_t)

        k2_s = deal(gather(dsc, k2_t, U8, "k2_sg"), U8, "k2_s")
        place_odd_rows(k2_s, nc.sync)
        k2_w = deal(gather(dwd, k2_t, U32, "k2_wg"), U32, "k2_w")
        two_w = gather(xwd, two_t, U32, "two_w")
        two_s = gather(xsc, two_t, U8, "two_s")
        b_ps = [psum.tile([P, S], F32, name=f"b{t}", tag=f"b{t}") for t in range(PACK)]
        for t in range(PACK):
            product(b_ps[t], k2_w, k2_s, t, two_w, two_s)
        for t in range(PACK):
            nc.scalar.activation(b_win[t][:, :S], b_ps[t][:], COPY, scale=0.03125)
        c_w = deal(gather(xwd, cand_t, U32, "c_wg"), U32, "c_w")
        c_s = deal(gather(xsc, cand_t, U8, "c_sg"), U8, "c_s")
        for t in range(PACK):
            nc.vector.tensor_tensor(ra[t][:], b_win[t][:, S : S + W], b_win[t][:, S + W :], MAX)
        for t in range(2):
            nc.scalar.activation(h_sb[t][:].indirect(n1_t[:]), ra[t][:], COPY)
        for t in range(2, 4):
            nc.vector.tensor_copy(h_sb[t][:].indirect(n1_t[:]), ra[t][:])
        for t in (2, 0, 3, 1):
            nc.vector.tensor_scalar(z16[:, t, :], h_sb[t][:], gs16[:, t : t + 1], None, MULT)

        def interleave(src, name, cols):
            dst = new([P, cols.stop - cols.start, PACK], BF16, name)
            nc.vector.tensor_copy(
                dst[:].rearrange("p (c i) t -> p c t i", i=4), src[:, :, cols].rearrange("p t (c i) -> p c t i", i=4)
            )
            return dst

        def quantize(src, name):
            words = new([P, S], U32, name + "_w")
            scales = new([P, S], U8, name + "_s")
            halves = [slice(0, W), slice(W, S)]
            woven = [interleave(src, f"{name}i{u}", cols) for u, cols in enumerate(halves)]
            for u, cols in enumerate(halves):
                nc.vector.quantize_mx(out=words[:, cols].bitcast(FP8X4), scales=scales[:, cols], in_=woven[u][:].rearrange("p c t -> p (c t)"))
            return words, scales

        z_w, z_s = quantize(z16, "z")

        a_win = [new([P, 2 * S], F32, f"awin{t}", tag) for t, tag in enumerate(("ra0", "ra1", "zi0", "zi1"))]
        for t in range(PACK):
            (sgather if t < 2 else vgather)(a_win[t][:, S:], b_win[t], n5_t)

        a_ps = [psum.tile([P, S], F32, name=f"a{t}", tag=f"ha{t}") for t in range(PACK)]
        for t in range(PACK):
            product(a_ps[t], c_w, c_s, t, z_w, z_s)

        y = new([P, PACK, S], F32, "y")
        out_rows = out_0.rearrange("(p t) j -> p t j", t=PACK)
        for t in range(PACK):
            nc.scalar.activation(a_win[t][:, :S], a_ps[t][:], COPY, scale=0.0625)
            g3 = new([P, S], F32, f"g3_{t}")
            g4 = new([P, S], F32, f"g4_{t}")
            sgather(g3[:], a_win[t], n3_t)
            sgather(g4[:], a_win[t], n4_t)
            nc.vector.scalar_tensor_tensor(g3[:], a_ps[t][:], -0.0625, g3[:], MULT, ADD)
            nc.vector.scalar_tensor_tensor(g4[:], a_ps[t][:], -0.0625, g4[:], MULT, ADD)
            nc.vector.scalar_tensor_tensor(g3[:], g3[:], 0.0625, b_ps[t][:], MULT, MULT)
            nc.vector.tensor_tensor(g4[:], g4[:], a_win[t][:, S:], MULT)
            nc.vector.tensor_tensor(y[:, t, :], g3[:], g4[:], ADD)
            nc.sync.dma_start(out_rows[:, t, :], y[:, t, :])

        y_w, y_s = quantize(y, "y")
        nc.sync.dma_start(out_1[0].rearrange("p n t -> p (n t)").bitcast(I32), y_w[:].bitcast(I32))
        for q in range(4):
            queue = nc.scalar if q % 2 else nc.sync
            queue.dma_start(out_2[0, 4 * q : 4 * q + 4, :].bitcast(I32), y_s[32 * q : 32 * q + 4, :].bitcast(I32))
